import numpy as np
import ml_dtypes


def mxq(x, axis, fmt="e4m3"):
    dtype, down = {"e4m3": (ml_dtypes.float8_e4m3fn, 7), "e5m2": (ml_dtypes.float8_e5m2, 14)}[fmt]
    v = np.moveaxis(np.asarray(x, np.float32).astype(ml_dtypes.bfloat16).astype(np.float64), axis, -1)
    blocks = v.reshape(v.shape[:-1] + (-1, 32))
    amax = np.abs(blocks).max(-1, keepdims=True)
    byte = np.maximum(np.where(amax > 0, np.frexp(amax)[1] - 1 + 127, 0) - down, 1)
    scale = np.exp2(byte - 127.0)
    codes = (blocks / scale).astype(np.float32).astype(dtype).astype(np.float64)
    return np.moveaxis((codes * scale).reshape(v.shape), -1, axis)


WIDE = False


def mx_kscale(k):
    if not WIDE:
        return np.ones(k)
    levels = np.array([10, -10, 5, -5, 0])
    if k % 512:
        return np.exp2(np.random.permutation(np.resize(levels, k // 32))).repeat(32)
    a = np.empty((k // 512, 16))
    for p in range(k // 512):
        a[p, :8] = np.random.permutation(np.resize(levels, 8))
        for g in range(8):
            far = levels[np.abs(levels - a[p, g]) >= 10]
            a[p, g + 8] = far[np.random.randint(len(far))]
    return np.exp2(a.ravel()).repeat(32)


def f64(x):
    return np.asarray(x).astype(np.float64)


def striped(idx):
    return np.tile(idx.reshape(-1, 16).T, (8, 1)).astype(np.uint16)


def unstriped(offs):
    return offs[:16].T.reshape(-1).astype(np.int64)


def relu2(v):
    return np.maximum(v, 0.0) ** 2


K, T, D, S, V, R, N = 512, 2048, 5, 1280, 256, 8, 128


def setup_inputs():
    n = np.random.standard_normal
    s = mx_kscale(K)[:, None]
    return {
        "xT": (n((K, T)) * s).astype(np.float32),
        "w": (n((D, K, N)) / np.sqrt(D * K) / s[None]).astype(np.float32),
        "b": (0.3 * n((N, 1))).astype(np.float32),
        "offs": striped(np.concatenate([R * np.arange(V) + np.random.randint(0, R, V) for _ in range(D)])),
    }


def reference(xT, w, b, offs):
    idx = unstriped(offs)
    xq = mxq(f64(xT)[:, idx], 0, "e4m3")
    wq = mxq(f64(w), 1, "e4m3")
    y = sum(wq[d].T @ xq[:, d * V:(d + 1) * V] for d in range(D))
    y = relu2(y + f64(b))
    return y

@@ -1,0 +1,116 @@
+from contextlib import ExitStack
+
+import concourse.mybir as mybir
+
+K, T, D, S, V, N = 512, 2048, 5, 1280, 256, 128
+FLOPS = 2 * N * V * D * K
+
+F32 = mybir.dt.float32
+BF16 = mybir.dt.bfloat16
+U32 = mybir.dt.uint32
+U16 = mybir.dt.uint16
+U8 = mybir.dt.uint8
+FP8X4 = mybir.dt.float8_e4m3fn_x4
+ADD = mybir.AluOpType.add
+MAX = mybir.AluOpType.max
+SQUARE = mybir.ActivationFunctionType.Square
+
+P = 128
+PACK = 4
+CHUNKS = [(0, 512, 192), (512, 512, 192), (1024, 512, 192), (1536, 256, 160), (1792, 256, 160)]
+W_PARTS = [(0, 2), (2, 4), (4, 5)]
+BYTE_PARTS = [(0, 2), (2, 4), (4, 5)]
+
+
+def tile_picked_deform_lin_relu2_def_e_kernel(tc, xT, w, b, offs, out):
+    nc = tc.nc
+    with ExitStack() as ctx:
+        keep = ctx.enter_context(tc.tile_pool(name="keep", bufs=1))
+        psum = ctx.enter_context(tc.psum_pool(name="psum", bufs=1))
+
+        offsets = keep.tile([P, S // 16], U16, name="offsets")
+        codes = keep.tile([P, T], U32, name="codes", align_bytes=64)
+        scales = keep.tile([P, T], U8, name="scales", align_bytes=64)
+        picked_codes = keep.tile([P, S], U32, name="picked_codes", align_bytes=64)
+        picked_scales = keep.tile([P, S], U8, name="picked_scales", align_bytes=64)
+        w_codes = keep.tile([P, D * N], U32, name="w_codes", align_bytes=64)
+        w_scales = keep.tile([P, D * N], U8, name="w_scales", align_bytes=64)
+        bias = keep.tile([P, 1], F32, name="bias")
+        sums = keep.tile([P, V], F32, name="sums")
+        result = keep.tile([P, V], F32, name="result")
+        acc = psum.tile([P, V], F32, name="acc")
+
+        nc.gpsimd.memset(scales[:], 0)
+
+        x_raw = []
+        for i, (c0, width, on_vector) in enumerate(CHUNKS):
+            raw = keep.tile([P, PACK, width], F32, name=f"x_raw{i}")
+            nc.sync.dma_start(out=raw[:], in_=xT[:, c0 : c0 + width].rearrange("(p j) c -> p j c", j=PACK))
+            x_raw.append(raw)
+            if i == 0:
+                nc.sync.dma_start(offsets[:], offs)
+        w_raw = []
+        for i, (d0, d1) in enumerate(W_PARTS):
+            raw = keep.tile([P, d1 - d0, PACK, N], F32, name=f"w_raw{i}")
+            nc.sync.dma_start(out=raw[:], in_=w[d0:d1].rearrange("d (p j) m -> p d j m", j=PACK))
+            w_raw.append(raw)
+        nc.sync.dma_start(out=bias[:], in_=b)
+
+        x_grouped = []
+
+        def quantize_chunk(i):
+            c0, width, on_vector = CHUNKS[i]
+            nc.vector.quantize_mx(
+                out=codes[:, c0 : c0 + width].bitcast(FP8X4),
+                scales=scales[:, c0 : c0 + width],
+                in_=x_grouped[i][:].rearrange("p c j -> p (c j)"),
+            )
+
+        for i, (c0, width, a) in enumerate(CHUNKS):
+            raw = x_raw[i]
+            grouped = keep.tile([P, width, PACK], BF16, name=f"x_grouped{i}", align_bytes=64)
+            nc.scalar.copy(out=grouped[:, a:width, :], in_=raw[:, :, a:width].rearrange("p j c -> p c j"))
+            nc.vector.tensor_copy(out=grouped[:, 0:a, :], in_=raw[:, :, 0:a].rearrange("p j c -> p c j"))
+            x_grouped.append(grouped)
+            if i > 0:
+                quantize_chunk(i - 1)
+        quantize_chunk(len(CHUNKS) - 1)
+
+        w_grouped = []
+        for i, (d0, d1) in enumerate(W_PARTS):
+            grouped = keep.tile([P, d1 - d0, N, PACK], BF16, name=f"w_grouped{i}", align_bytes=64)
+            for d in range(d0, d1):
+                nc.scalar.copy(out=grouped[:, d - d0], in_=w_raw[i][:, d - d0].rearrange("p j m -> p m j"))
+            w_grouped.append(grouped)
+
+        nc.vector.tensor_copy(out=picked_codes[:], in_=codes[:].indirect(offsets[:]))
+        for i, (d0, d1) in enumerate(W_PARTS):
+            m_cols = slice(d0 * N, d1 * N)
+            nc.vector.quantize_mx(
+                out=w_codes[:, m_cols].bitcast(FP8X4),
+                scales=w_scales[:, m_cols],
+                in_=w_grouped[i][:].rearrange("p d m j -> p (d m j)"),
+            )
+        for d0, d1 in BYTE_PARTS:
+            list_cols = slice(d0 * V // 16, d1 * V // 16)
+            nc.vector.tensor_copy(
+                out=picked_scales[:, d0 * V : d1 * V], in_=scales[:].indirect(offsets[:, list_cols])
+            )
+            for d in range(d0, d1):
+                m_cols = slice(d * N, (d + 1) * N)
+                v_cols = slice(d * V, (d + 1) * V)
+                nc.tensor.matmul_mx(
+                    out=acc[:],
+                    lhsT=w_codes[:, m_cols].bitcast(FP8X4),
+                    lhsT_scale=w_scales[:, m_cols],
+                    rhs=picked_codes[:, v_cols].bitcast(FP8X4),
+                    rhs_scale=picked_scales[:, v_cols],
+                    start=(d == 0),
+                    stop=(d == D - 1),
+                )
+
+        for v0 in range(0, V, V // 2):
+            half = slice(v0, v0 + V // 2)
+            nc.vector.tensor_scalar(sums[:, half], acc[:, half], bias[:], 0.0, ADD, MAX)
+            nc.scalar.activation(result[:, half], sums[:, half], SQUARE)
+        nc.scalar.dma_start(out=out, in_=result[:])

@@ -8,6 +8,7 @@ FLOPS = 2 * N * V * D * K
 F32 = mybir.dt.float32
 BF16 = mybir.dt.bfloat16
 U32 = mybir.dt.uint32
+I32 = mybir.dt.int32
 U16 = mybir.dt.uint16
 U8 = mybir.dt.uint8
 FP8X4 = mybir.dt.float8_e4m3fn_x4
@@ -17,9 +18,21 @@ SQUARE = mybir.ActivationFunctionType.Square
 
 P = 128
 PACK = 4
-CHUNKS = [(0, 512, 192), (512, 512, 192), (1024, 512, 192), (1536, 256, 160), (1792, 256, 160)]
+CHUNKS = [
+    (0, 0, 1024, 640),
+    (0, 1024, 512, 320),
+    (0, 1536, 512, 320),
+    (1, 0, 512, 0),
+    (1, 512, 512, 0),
+    (1, 1024, 512, 0),
+    (1, 1536, 512, 320),
+]
+EARLY = 128
+EARLY_WINDOW = 8 * EARLY
+EARLY_SLICES = [(0, EARLY), (2 * V, 2 * V + EARLY)]
+LATE_SLICES = [(EARLY, 2 * V), (2 * V + EARLY, S)]
 W_PARTS = [(0, 2), (2, 4), (4, 5)]
-BYTE_PARTS = [(0, 2), (2, 4), (4, 5)]
+X_PARTS = [(3, 5), (0, 1), (1, 2), (2, 3)]
 
 
 def tile_picked_deform_lin_relu2_def_e_kernel(tc, xT, w, b, offs, out):
@@ -29,10 +42,10 @@ def tile_picked_deform_lin_relu2_def_e_kernel(tc, xT, w, b, offs, out):
         psum = ctx.enter_context(tc.psum_pool(name="psum", bufs=1))
 
         offsets = keep.tile([P, S // 16], U16, name="offsets")
-        codes = keep.tile([P, T], U32, name="codes", align_bytes=64)
-        scales = keep.tile([P, T], U8, name="scales", align_bytes=64)
-        picked_codes = keep.tile([P, S], U32, name="picked_codes", align_bytes=64)
-        picked_scales = keep.tile([P, S], U8, name="picked_scales", align_bytes=64)
+        pairs = [keep.tile([P, T], U32, name=f"pairs{u}", align_bytes=64) for u in range(2)]
+        picked = keep.tile([P, 2, S], U32, name="picked", align_bytes=64)
+        x_codes = keep.tile([P, S], U32, name="x_codes", align_bytes=64)
+        x_scales = keep.tile([P, S], U8, name="x_scales", align_bytes=64)
         w_codes = keep.tile([P, D * N], U32, name="w_codes", align_bytes=64)
         w_scales = keep.tile([P, D * N], U8, name="w_scales", align_bytes=64)
         bias = keep.tile([P, 1], F32, name="bias")
@@ -40,50 +53,49 @@ def tile_picked_deform_lin_relu2_def_e_kernel(tc, xT, w, b, offs, out):
         result = keep.tile([P, V], F32, name="result")
         acc = psum.tile([P, V], F32, name="acc")
 
-        nc.gpsimd.memset(scales[:], 0)
-
+        x_rows = xT.rearrange("(p j) c -> p j c", j=PACK)
         x_raw = []
-        for i, (c0, width, on_vector) in enumerate(CHUNKS):
-            raw = keep.tile([P, PACK, width], F32, name=f"x_raw{i}")
-            nc.sync.dma_start(out=raw[:], in_=xT[:, c0 : c0 + width].rearrange("(p j) c -> p j c", j=PACK))
+        for i, (u, c0, width, on_vector) in enumerate(CHUNKS):
+            raw = keep.tile([P, 2, width], F32, name=f"x_raw{i}")
+            nc.sync.dma_start(out=raw[:], in_=x_rows[:, 2 * u : 2 * u + 2, c0 : c0 + width])
             x_raw.append(raw)
             if i == 0:
                 nc.sync.dma_start(offsets[:], offs)
         w_raw = []
-        for i, (d0, d1) in enumerate(W_PARTS):
-            raw = keep.tile([P, d1 - d0, PACK, N], F32, name=f"w_raw{i}")
-            nc.sync.dma_start(out=raw[:], in_=w[d0:d1].rearrange("d (p j) m -> p d j m", j=PACK))
+        for d in range(D):
+            raw = keep.tile([P, PACK, N], F32, name=f"w_raw{d}", tag=f"w_slot{d}", align_bytes=64)
+            nc.sync.dma_start(out=raw[:], in_=w[d].rearrange("(p j) m -> p j m", j=PACK))
             w_raw.append(raw)
         nc.sync.dma_start(out=bias[:], in_=b)
 
-        x_grouped = []
+        def gather(u, slices, window):
+            for e0, e1 in slices:
+                nc.vector.tensor_copy(
+                    out=picked[:, u, e0:e1], in_=pairs[u][:, 0:window].indirect(offsets[:, e0 // 16 : e1 // 16])
+                )
 
-        def quantize_chunk(i):
-            c0, width, on_vector = CHUNKS[i]
-            nc.vector.quantize_mx(
-                out=codes[:, c0 : c0 + width].bitcast(FP8X4),
-                scales=scales[:, c0 : c0 + width],
-                in_=x_grouped[i][:].rearrange("p c j -> p (c j)"),
-            )
-
-        for i, (c0, width, a) in enumerate(CHUNKS):
+        for i, (u, c0, width, a) in enumerate(CHUNKS):
             raw = x_raw[i]
-            grouped = keep.tile([P, width, PACK], BF16, name=f"x_grouped{i}", align_bytes=64)
-            nc.scalar.copy(out=grouped[:, a:width, :], in_=raw[:, :, a:width].rearrange("p j c -> p c j"))
-            nc.vector.tensor_copy(out=grouped[:, 0:a, :], in_=raw[:, :, 0:a].rearrange("p j c -> p c j"))
-            x_grouped.append(grouped)
-            if i > 0:
-                quantize_chunk(i - 1)
-        quantize_chunk(len(CHUNKS) - 1)
+            nc.scalar.copy(
+                out=pairs[u][:, c0 + a : c0 + width].bitcast(BF16).rearrange("p (c j) -> p c j", j=2),
+                in_=raw[:, :, a:width].rearrange("p j c -> p c j"),
+            )
+            if a > 0:
+                nc.vector.tensor_copy(
+                    out=pairs[u][:, c0 : c0 + a].bitcast(BF16).rearrange("p (c j) -> p c j", j=2),
+                    in_=raw[:, :, 0:a].rearrange("p j c -> p c j"),
+                )
+            if c0 + width == EARLY_WINDOW:
+                gather(u, EARLY_SLICES, EARLY_WINDOW)
+            if c0 + width == T:
+                gather(u, LATE_SLICES, T)
 
         w_grouped = []
         for i, (d0, d1) in enumerate(W_PARTS):
             grouped = keep.tile([P, d1 - d0, N, PACK], BF16, name=f"w_grouped{i}", align_bytes=64)
             for d in range(d0, d1):
-                nc.scalar.copy(out=grouped[:, d - d0], in_=w_raw[i][:, d - d0].rearrange("p j m -> p m j"))
+                nc.scalar.copy(out=grouped[:, d - d0], in_=w_raw[d][:].rearrange("p j m -> p m j"))
             w_grouped.append(grouped)
-
-        nc.vector.tensor_copy(out=picked_codes[:], in_=codes[:].indirect(offsets[:]))
         for i, (d0, d1) in enumerate(W_PARTS):
             m_cols = slice(d0 * N, d1 * N)
             nc.vector.quantize_mx(
@@ -91,10 +103,23 @@ def tile_picked_deform_lin_relu2_def_e_kernel(tc, xT, w, b, offs, out):
                 scales=w_scales[:, m_cols],
                 in_=w_grouped[i][:].rearrange("p d m j -> p (d m j)"),
             )
-        for d0, d1 in BYTE_PARTS:
-            list_cols = slice(d0 * V // 16, d1 * V // 16)
-            nc.vector.tensor_copy(
-                out=picked_scales[:, d0 * V : d1 * V], in_=scales[:].indirect(offsets[:, list_cols])
+
+        for d0, d1 in X_PARTS:
+            entries = slice(d0 * V, d1 * V)
+            if d1 == D:
+                grouped = keep.tile([P, 2 * (d1 - d0) * V], U32, name="x_grouped_last", align_bytes=64)
+                nc.vector.tensor_copy(
+                    out=grouped[:].bitcast(I32).rearrange("p (v u) -> p v u", u=2),
+                    in_=picked[:, :, entries].bitcast(I32).rearrange("p u v -> p v u"),
+                )
+            else:
+                grouped = keep.tile([P, 2 * V], U32, name=f"x_grouped{d0}", tag=f"w_slot{D - 1 - d0}", align_bytes=64)
+                nc.scalar.copy(
+                    out=grouped[:].rearrange("p (v u) -> p v u", u=2),
+                    in_=picked[:, :, entries].rearrange("p u v -> p v u"),
+                )
+            nc.vector.quantize_mx(
+                out=x_codes[:, entries].bitcast(FP8X4), scales=x_scales[:, entries], in_=grouped[:].bitcast(BF16)
             )
             for d in range(d0, d1):
                 m_cols = slice(d * N, (d + 1) * N)
@@ -103,10 +128,10 @@ def tile_picked_deform_lin_relu2_def_e_kernel(tc, xT, w, b, offs, out):
                     out=acc[:],
                     lhsT=w_codes[:, m_cols].bitcast(FP8X4),
                     lhsT_scale=w_scales[:, m_cols],
-                    rhs=picked_codes[:, v_cols].bitcast(FP8X4),
-                    rhs_scale=picked_scales[:, v_cols],
-                    start=(d == 0),
-                    stop=(d == D - 1),
+                    rhs=x_codes[:, v_cols].bitcast(FP8X4),
+                    rhs_scale=x_scales[:, v_cols],
+                    start=(d == X_PARTS[0][0]),
+                    stop=(d == X_PARTS[-1][1] - 1),
                 )
 
         for v0 in range(0, V, V // 2):

@@ -29,10 +29,11 @@ CHUNKS = [
 ]
 EARLY = 128
 EARLY_WINDOW = 8 * EARLY
-EARLY_SLICES = [(0, EARLY), (2 * V, 2 * V + EARLY)]
-LATE_SLICES = [(EARLY, 2 * V), (2 * V + EARLY, S)]
+EARLY_SLICES = [(0, EARLY, 0), (2 * V, 2 * V + EARLY, EARLY)]
+LATE_SLICES = [(EARLY, 2 * V, 2 * EARLY), (2 * V + EARLY, S, 2 * V + EARLY)]
+H = V // 2
+RELU = mybir.ActivationFunctionType.Relu
 W_PARTS = [(0, 2), (2, 4), (4, 5)]
-X_PARTS = [(3, 5), (0, 1), (1, 2), (2, 3)]
 
 
 def tile_picked_deform_lin_relu2_def_e_kernel(tc, xT, w, b, offs, out):
@@ -51,7 +52,7 @@ def tile_picked_deform_lin_relu2_def_e_kernel(tc, xT, w, b, offs, out):
         bias = keep.tile([P, 1], F32, name="bias")
         sums = keep.tile([P, V], F32, name="sums")
         result = keep.tile([P, V], F32, name="result")
-        acc = psum.tile([P, V], F32, name="acc")
+        acc = [psum.tile([P, H], F32, name=f"acc{h}") for h in range(2)]
 
         x_rows = xT.rearrange("(p j) c -> p j c", j=PACK)
         x_raw = []
@@ -69,10 +70,21 @@ def tile_picked_deform_lin_relu2_def_e_kernel(tc, xT, w, b, offs, out):
         nc.sync.dma_start(out=bias[:], in_=b)
 
         def gather(u, slices, window):
-            for e0, e1 in slices:
+            for e0, e1, c0 in slices:
                 nc.vector.tensor_copy(
-                    out=picked[:, u, e0:e1], in_=pairs[u][:, 0:window].indirect(offsets[:, e0 // 16 : e1 // 16])
+                    out=picked[:, u, c0 : c0 + e1 - e0], in_=pairs[u][:, 0:window].indirect(offsets[:, e0 // 16 : e1 // 16])
                 )
+
+        def weave_on_vector(dst, src):
+            nc.vector.tensor_copy(
+                out=dst.bitcast(I32).rearrange("p (v u) -> p v u", u=2), in_=src.bitcast(I32).rearrange("p u v -> p v u")
+            )
+
+        def quantize(first, count, grouped):
+            cols = slice(first * H, (first + count) * H)
+            nc.vector.quantize_mx(
+                out=x_codes[:, cols].bitcast(FP8X4), scales=x_scales[:, cols], in_=grouped[:].bitcast(BF16)
+            )
 
         for i, (u, c0, width, a) in enumerate(CHUNKS):
             raw = x_raw[i]
@@ -87,6 +99,10 @@ def tile_picked_deform_lin_relu2_def_e_kernel(tc, xT, w, b, offs, out):
                 )
             if c0 + width == EARLY_WINDOW:
                 gather(u, EARLY_SLICES, EARLY_WINDOW)
+                if u == 1:
+                    early = keep.tile([P, 4 * H], U32, name="x_early", align_bytes=64)
+                    weave_on_vector(early[:], picked[:, :, 0 : 2 * H])
+                    quantize(0, 2, early)
             if c0 + width == T:
                 gather(u, LATE_SLICES, T)
 
@@ -94,7 +110,10 @@ def tile_picked_deform_lin_relu2_def_e_kernel(tc, xT, w, b, offs, out):
         for i, (d0, d1) in enumerate(W_PARTS):
             grouped = keep.tile([P, d1 - d0, N, PACK], BF16, name=f"w_grouped{i}", align_bytes=64)
             for d in range(d0, d1):
-                nc.scalar.copy(out=grouped[:, d - d0], in_=w_raw[d][:].rearrange("p j m -> p m j"))
+                nc.scalar.copy(
+                    out=grouped[:, d - d0].rearrange("p (c i) j -> p c j i", i=4),
+                    in_=w_raw[d][:].rearrange("p j (c i) -> p c j i", i=4),
+                )
             w_grouped.append(grouped)
         for i, (d0, d1) in enumerate(W_PARTS):
             m_cols = slice(d0 * N, d1 * N)
@@ -104,38 +123,35 @@ def tile_picked_deform_lin_relu2_def_e_kernel(tc, xT, w, b, offs, out):
                 in_=w_grouped[i][:].rearrange("p d m j -> p (d m j)"),
             )
 
-        for d0, d1 in X_PARTS:
-            entries = slice(d0 * V, d1 * V)
-            if d1 == D:
-                grouped = keep.tile([P, 2 * (d1 - d0) * V], U32, name="x_grouped_last", align_bytes=64)
-                nc.vector.tensor_copy(
-                    out=grouped[:].bitcast(I32).rearrange("p (v u) -> p v u", u=2),
-                    in_=picked[:, :, entries].bitcast(I32).rearrange("p u v -> p v u"),
-                )
-            else:
-                grouped = keep.tile([P, 2 * V], U32, name=f"x_grouped{d0}", tag=f"w_slot{D - 1 - d0}", align_bytes=64)
-                nc.scalar.copy(
-                    out=grouped[:].rearrange("p (v u) -> p v u", u=2),
-                    in_=picked[:, :, entries].rearrange("p u v -> p v u"),
-                )
-            nc.vector.quantize_mx(
-                out=x_codes[:, entries].bitcast(FP8X4), scales=x_scales[:, entries], in_=grouped[:].bitcast(BF16)
-            )
-            for d in range(d0, d1):
+        blocks = picked[:].rearrange("p u (g v) -> p g v u", v=H)
+        on_vector = keep.tile([P, 4 * H], U32, name="x_on_vector", align_bytes=64)
+        nc.vector.tensor_copy(
+            out=on_vector[:].bitcast(I32).rearrange("p (g v u) -> p g v u", g=2, u=2),
+            in_=picked[:].bitcast(I32).rearrange("p u (g v) -> p g v u", v=H)[:, 6:9:2],
+        )
+        quantize(2, 2, on_vector)
+        for i, src in enumerate([blocks[:, 2:4], blocks[:, 4:6], blocks[:, 7:10:2]]):
+            grouped = keep.tile([P, 4 * H], U32, name=f"x_on_scalar{i}", tag=f"w_slot{2 + i}", align_bytes=64)
+            nc.scalar.copy(out=grouped[:].rearrange("p (g v u) -> p g v u", g=2, u=2), in_=src)
+            quantize(4 + 2 * i, 2, grouped)
+
+        for h, taps in enumerate([[(0, 0), (2, 1), (3, 2), (4, 3), (1, 5)], [(0, 4), (1, 6), (2, 7), (3, 8), (4, 9)]]):
+            for i, (d, block) in enumerate(taps):
                 m_cols = slice(d * N, (d + 1) * N)
-                v_cols = slice(d * V, (d + 1) * V)
+                cols = slice(block * H, (block + 1) * H)
                 nc.tensor.matmul_mx(
-                    out=acc[:],
+                    out=acc[h][:],
                     lhsT=w_codes[:, m_cols].bitcast(FP8X4),
                     lhsT_scale=w_scales[:, m_cols],
-                    rhs=x_codes[:, v_cols].bitcast(FP8X4),
-                    rhs_scale=x_scales[:, v_cols],
-                    start=(d == X_PARTS[0][0]),
-                    stop=(d == X_PARTS[-1][1] - 1),
+                    rhs=x_codes[:, cols].bitcast(FP8X4),
+                    rhs_scale=x_scales[:, cols],
+                    start=(i == 0),
+                    stop=(i == D - 1),
                 )
 
-        for v0 in range(0, V, V // 2):
-            half = slice(v0, v0 + V // 2)
-            nc.vector.tensor_scalar(sums[:, half], acc[:, half], bias[:], 0.0, ADD, MAX)
-            nc.scalar.activation(result[:, half], sums[:, half], SQUARE)
-        nc.scalar.dma_start(out=out, in_=result[:])
+        nc.scalar.activation(sums[:, 0:H], acc[0][:], RELU, bias=bias[:])
+        nc.scalar.activation(result[:, 0:H], sums[:, 0:H], SQUARE)
+        nc.sync.dma_start(out=out[:, 0:H], in_=result[:, 0:H])
+        nc.vector.tensor_scalar(sums[:, H:V], acc[1][:], bias[:], 0.0, ADD, MAX)
+        nc.scalar.activation(result[:, H:V], sums[:, H:V], SQUARE)
+        nc.scalar.dma_start(out=out[:, H:V], in_=result[:, H:V])

@@ -20,8 +20,8 @@ P = 128
 PACK = 4
 CHUNKS = [
     (0, 0, 1024, 640),
-    (0, 1024, 512, 320),
-    (0, 1536, 512, 320),
+    (0, 1024, 768, 480),
+    (0, 1792, 256, 160),
     (1, 0, 512, 0),
     (1, 512, 512, 0),
     (1, 1024, 512, 0),
@@ -30,7 +30,7 @@ CHUNKS = [
 EARLY = 128
 EARLY_WINDOW = 8 * EARLY
 EARLY_SLICES = [(0, EARLY, 0), (2 * V, 2 * V + EARLY, EARLY)]
-LATE_SLICES = [(EARLY, 2 * V, 2 * EARLY), (2 * V + EARLY, S, 2 * V + EARLY)]
+LATE_SLICES = [(2 * V + EARLY, S, 2 * V + EARLY), (EARLY, 2 * V, 2 * EARLY)]
 H = V // 2
 RELU = mybir.ActivationFunctionType.Relu
 W_PARTS = [(0, 2), (2, 4), (4, 5)]
@@ -49,6 +49,7 @@ def tile_picked_deform_lin_relu2_def_e_kernel(tc, xT, w, b, offs, out):
         x_scales = keep.tile([P, S], U8, name="x_scales", align_bytes=64)
         w_codes = keep.tile([P, D * N], U32, name="w_codes", align_bytes=64)
         w_scales = keep.tile([P, D * N], U8, name="w_scales", align_bytes=64)
+        on_vector = keep.tile([P, 8 * H], U32, name="x_on_vector", align_bytes=64)
         bias = keep.tile([P, 1], F32, name="bias")
         sums = keep.tile([P, V], F32, name="sums")
         result = keep.tile([P, V], F32, name="result")
@@ -56,7 +57,7 @@ def tile_picked_deform_lin_relu2_def_e_kernel(tc, xT, w, b, offs, out):
 
         x_rows = xT.rearrange("(p j) c -> p j c", j=PACK)
         x_raw = []
-        for i, (u, c0, width, on_vector) in enumerate(CHUNKS):
+        for i, (u, c0, width, share) in enumerate(CHUNKS):
             raw = keep.tile([P, 2, width], F32, name=f"x_raw{i}")
             nc.sync.dma_start(out=raw[:], in_=x_rows[:, 2 * u : 2 * u + 2, c0 : c0 + width])
             x_raw.append(raw)
@@ -100,9 +101,8 @@ def tile_picked_deform_lin_relu2_def_e_kernel(tc, xT, w, b, offs, out):
             if c0 + width == EARLY_WINDOW:
                 gather(u, EARLY_SLICES, EARLY_WINDOW)
                 if u == 1:
-                    early = keep.tile([P, 4 * H], U32, name="x_early", align_bytes=64)
-                    weave_on_vector(early[:], picked[:, :, 0 : 2 * H])
-                    quantize(0, 2, early)
+                    for g in range(2):
+                        weave_on_vector(on_vector[:, 2 * g * H : 2 * (g + 1) * H], picked[:, :, g * H : (g + 1) * H])
             if c0 + width == T:
                 gather(u, LATE_SLICES, T)
 
@@ -124,18 +124,17 @@ def tile_picked_deform_lin_relu2_def_e_kernel(tc, xT, w, b, offs, out):
             )
 
         blocks = picked[:].rearrange("p u (g v) -> p g v u", v=H)
-        on_vector = keep.tile([P, 4 * H], U32, name="x_on_vector", align_bytes=64)
         nc.vector.tensor_copy(
-            out=on_vector[:].bitcast(I32).rearrange("p (g v u) -> p g v u", g=2, u=2),
+            out=on_vector[:, 4 * H : 8 * H].bitcast(I32).rearrange("p (g v u) -> p g v u", g=2, u=2),
             in_=picked[:].bitcast(I32).rearrange("p u (g v) -> p g v u", v=H)[:, 6:9:2],
         )
-        quantize(2, 2, on_vector)
-        for i, src in enumerate([blocks[:, 2:4], blocks[:, 4:6], blocks[:, 7:10:2]]):
+        quantize(0, 4, on_vector)
+        for i, src in enumerate([blocks[:, 7:10:2], blocks[:, 2:4], blocks[:, 4:6]]):
             grouped = keep.tile([P, 4 * H], U32, name=f"x_on_scalar{i}", tag=f"w_slot{2 + i}", align_bytes=64)
             nc.scalar.copy(out=grouped[:].rearrange("p (g v u) -> p g v u", g=2, u=2), in_=src)
             quantize(4 + 2 * i, 2, grouped)
 
-        for h, taps in enumerate([[(0, 0), (2, 1), (3, 2), (4, 3), (1, 5)], [(0, 4), (1, 6), (2, 7), (3, 8), (4, 9)]]):
+        for h, taps in enumerate([[(0, 0), (2, 1), (3, 2), (4, 3), (1, 7)], [(3, 4), (4, 5), (0, 6), (1, 8), (2, 9)]]):
             for i, (d, block) in enumerate(taps):
                 m_cols = slice(d * N, (d + 1) * N)
                 cols = slice(block * H, (block + 1) * H)

@@ -19,9 +19,9 @@ SQUARE = mybir.ActivationFunctionType.Square
 P = 128
 PACK = 4
 CHUNKS = [
-    (0, 0, 1024, 640),
-    (0, 1024, 768, 480),
-    (0, 1792, 256, 160),
+    (0, 0, 1024, 1024),
+    (0, 1024, 512, 0),
+    (0, 1536, 512, 384),
     (1, 0, 512, 0),
     (1, 512, 512, 0),
     (1, 1024, 512, 0),
@@ -32,6 +32,8 @@ EARLY_WINDOW = 8 * EARLY
 EARLY_SLICES = [(0, EARLY, 0), (2 * V, 2 * V + EARLY, EARLY)]
 LATE_SLICES = [(2 * V + EARLY, S, 2 * V + EARLY), (EARLY, 2 * V, 2 * EARLY)]
 H = V // 2
+W_RAW_AT = [0, 2048, 4096, 6144, 9216]
+WOVEN_AT = [6144, 8192, 10240]
 RELU = mybir.ActivationFunctionType.Relu
 W_PARTS = [(0, 2), (2, 4), (4, 5)]
 
@@ -40,6 +42,7 @@ def tile_picked_deform_lin_relu2_def_e_kernel(tc, xT, w, b, offs, out):
     nc = tc.nc
     with ExitStack() as ctx:
         keep = ctx.enter_context(tc.tile_pool(name="keep", bufs=1))
+        shared = ctx.enter_context(tc.tile_pool(name="shared", bufs=1))
         psum = ctx.enter_context(tc.psum_pool(name="psum", bufs=1))
 
         offsets = keep.tile([P, S // 16], U16, name="offsets")
@@ -57,15 +60,14 @@ def tile_picked_deform_lin_relu2_def_e_kernel(tc, xT, w, b, offs, out):
 
         x_rows = xT.rearrange("(p j) c -> p j c", j=PACK)
         x_raw = []
+        nc.sync.dma_start(offsets[:], offs)
         for i, (u, c0, width, share) in enumerate(CHUNKS):
             raw = keep.tile([P, 2, width], F32, name=f"x_raw{i}")
             nc.sync.dma_start(out=raw[:], in_=x_rows[:, 2 * u : 2 * u + 2, c0 : c0 + width])
             x_raw.append(raw)
-            if i == 0:
-                nc.sync.dma_start(offsets[:], offs)
         w_raw = []
         for d in range(D):
-            raw = keep.tile([P, PACK, N], F32, name=f"w_raw{d}", tag=f"w_slot{d}", align_bytes=64)
+            raw = shared.tile([P, PACK, N], F32, name=f"w_raw{d}", offset=W_RAW_AT[d], align_bytes=64)
             nc.sync.dma_start(out=raw[:], in_=w[d].rearrange("(p j) m -> p j m", j=PACK))
             w_raw.append(raw)
         nc.sync.dma_start(out=bias[:], in_=b)
@@ -89,10 +91,11 @@ def tile_picked_deform_lin_relu2_def_e_kernel(tc, xT, w, b, offs, out):
 
         for i, (u, c0, width, a) in enumerate(CHUNKS):
             raw = x_raw[i]
-            nc.scalar.copy(
-                out=pairs[u][:, c0 + a : c0 + width].bitcast(BF16).rearrange("p (c j) -> p c j", j=2),
-                in_=raw[:, :, a:width].rearrange("p j c -> p c j"),
-            )
+            if a < width:
+                nc.scalar.copy(
+                    out=pairs[u][:, c0 + a : c0 + width].bitcast(BF16).rearrange("p (c j) -> p c j", j=2),
+                    in_=raw[:, :, a:width].rearrange("p j c -> p c j"),
+                )
             if a > 0:
                 nc.vector.tensor_copy(
                     out=pairs[u][:, c0 : c0 + a].bitcast(BF16).rearrange("p (c j) -> p c j", j=2),
@@ -128,9 +131,12 @@ def tile_picked_deform_lin_relu2_def_e_kernel(tc, xT, w, b, offs, out):
             out=on_vector[:, 4 * H : 8 * H].bitcast(I32).rearrange("p (g v u) -> p g v u", g=2, u=2),
             in_=picked[:].bitcast(I32).rearrange("p u (g v) -> p g v u", v=H)[:, 6:9:2],
         )
-        quantize(0, 4, on_vector)
+        first_codes = shared.tile([P, 4 * H], U32, name="first_codes", offset=W_RAW_AT[2], align_bytes=64)
+        nc.vector.quantize_mx(
+            out=first_codes[:].bitcast(FP8X4), scales=x_scales[:, 0 : 4 * H], in_=on_vector[:].bitcast(BF16)
+        )
         for i, src in enumerate([blocks[:, 7:10:2], blocks[:, 2:4], blocks[:, 4:6]]):
-            grouped = keep.tile([P, 4 * H], U32, name=f"x_on_scalar{i}", tag=f"w_slot{2 + i}", align_bytes=64)
+            grouped = shared.tile([P, 4 * H], U32, name=f"x_on_scalar{i}", offset=WOVEN_AT[i], align_bytes=64)
             nc.scalar.copy(out=grouped[:].rearrange("p (g v u) -> p g v u", g=2, u=2), in_=src)
             quantize(4 + 2 * i, 2, grouped)
 
@@ -142,7 +148,7 @@ def tile_picked_deform_lin_relu2_def_e_kernel(tc, xT, w, b, offs, out):
                     out=acc[h][:],
                     lhsT=w_codes[:, m_cols].bitcast(FP8X4),
                     lhsT_scale=w_scales[:, m_cols],
-                    rhs=x_codes[:, cols].bitcast(FP8X4),
+                    rhs=(first_codes if block < 4 else x_codes)[:, cols].bitcast(FP8X4),
                     rhs_scale=x_scales[:, cols],
                     start=(i == 0),
                     stop=(i == D - 1),

@@ -33,6 +33,7 @@ EARLY_SLICES = [(0, EARLY, 0), (2 * V, 2 * V + EARLY, EARLY)]
 LATE_SLICES = [(2 * V + EARLY, S, 2 * V + EARLY), (EARLY, 2 * V, 2 * EARLY)]
 H = V // 2
 W_RAW_AT = [0, 2048, 4096, 6144, 9216]
+X_RAW_AT = 12288
 WOVEN_AT = [6144, 8192, 10240]
 RELU = mybir.ActivationFunctionType.Relu
 W_PARTS = [(0, 2), (2, 4), (4, 5)]
@@ -62,7 +63,10 @@ def tile_picked_deform_lin_relu2_def_e_kernel(tc, xT, w, b, offs, out):
         x_raw = []
         nc.sync.dma_start(offsets[:], offs)
         for i, (u, c0, width, share) in enumerate(CHUNKS):
-            raw = keep.tile([P, 2, width], F32, name=f"x_raw{i}")
+            if i == len(CHUNKS) - 2:
+                raw = shared.tile([P, 2, width], F32, name=f"x_raw{i}", offset=X_RAW_AT, align_bytes=64)
+            else:
+                raw = keep.tile([P, 2, width], F32, name=f"x_raw{i}")
             nc.sync.dma_start(out=raw[:], in_=x_rows[:, 2 * u : 2 * u + 2, c0 : c0 + width])
             x_raw.append(raw)
         w_raw = []
@@ -86,7 +90,7 @@ def tile_picked_deform_lin_relu2_def_e_kernel(tc, xT, w, b, offs, out):
         def quantize(first, count, grouped):
             cols = slice(first * H, (first + count) * H)
             nc.vector.quantize_mx(
-                out=x_codes[:, cols].bitcast(FP8X4), scales=x_scales[:, cols], in_=grouped[:].bitcast(BF16)
+                out=x_codes[:, cols].bitcast(FP8X4), scales=x_scales[:, cols], in_=grouped.bitcast(BF16)
             )
 
         for i, (u, c0, width, a) in enumerate(CHUNKS):
@@ -107,6 +111,13 @@ def tile_picked_deform_lin_relu2_def_e_kernel(tc, xT, w, b, offs, out):
                     for g in range(2):
                         weave_on_vector(on_vector[:, 2 * g * H : 2 * (g + 1) * H], picked[:, :, g * H : (g + 1) * H])
             if c0 + width == T:
+                if u == 1:
+                    early_codes = shared.tile([P, 2 * H], U32, name="early_codes", offset=X_RAW_AT, align_bytes=64)
+                    nc.vector.quantize_mx(
+                        out=early_codes[:].bitcast(FP8X4),
+                        scales=x_scales[:, 0 : 2 * H],
+                        in_=on_vector[:, 0 : 4 * H].bitcast(BF16),
+                    )
                 gather(u, LATE_SLICES, T)
 
         w_grouped = []
@@ -133,12 +144,18 @@ def tile_picked_deform_lin_relu2_def_e_kernel(tc, xT, w, b, offs, out):
         )
         first_codes = shared.tile([P, 4 * H], U32, name="first_codes", offset=W_RAW_AT[2], align_bytes=64)
         nc.vector.quantize_mx(
-            out=first_codes[:].bitcast(FP8X4), scales=x_scales[:, 0 : 4 * H], in_=on_vector[:].bitcast(BF16)
+            out=first_codes[:, 2 * H : 4 * H].bitcast(FP8X4),
+            scales=x_scales[:, 2 * H : 4 * H],
+            in_=on_vector[:, 4 * H : 8 * H].bitcast(BF16),
         )
         for i, src in enumerate([blocks[:, 7:10:2], blocks[:, 2:4], blocks[:, 4:6]]):
             grouped = shared.tile([P, 4 * H], U32, name=f"x_on_scalar{i}", offset=WOVEN_AT[i], align_bytes=64)
             nc.scalar.copy(out=grouped[:].rearrange("p (g v u) -> p g v u", g=2, u=2), in_=src)
-            quantize(4 + 2 * i, 2, grouped)
+            if i < 2:
+                quantize(4 + 2 * i, 2, grouped[:])
+            else:
+                quantize(8, 1, grouped[:, 0 : 2 * H])
+                quantize(9, 1, grouped[:, 2 * H : 4 * H])
 
         for h, taps in enumerate([[(0, 0), (2, 1), (3, 2), (4, 3), (1, 7)], [(3, 4), (4, 5), (0, 6), (1, 8), (2, 9)]]):
             for i, (d, block) in enumerate(taps):
@@ -148,7 +165,7 @@ def tile_picked_deform_lin_relu2_def_e_kernel(tc, xT, w, b, offs, out):
                     out=acc[h][:],
                     lhsT=w_codes[:, m_cols].bitcast(FP8X4),
                     lhsT_scale=w_scales[:, m_cols],
-                    rhs=(first_codes if block < 4 else x_codes)[:, cols].bitcast(FP8X4),
+                    rhs=(early_codes if block < 2 else first_codes if block < 4 else x_codes)[:, cols].bitcast(FP8X4),
                     rhs_scale=x_scales[:, cols],
                     start=(i == 0),
                     stop=(i == D - 1),

@@ -20,8 +20,7 @@ P = 128
 PACK = 4
 CHUNKS = [
     (0, 0, 1024, 1024),
-    (0, 1024, 512, 0),
-    (0, 1536, 512, 384),
+    (0, 1024, 1024, 704),
     (1, 0, 512, 0),
     (1, 512, 512, 0),
     (1, 1024, 512, 0),

@@ -175,4 +175,4 @@ def tile_picked_deform_lin_relu2_def_e_kernel(tc, xT, w, b, offs, out):
         nc.sync.dma_start(out=out[:, 0:H], in_=result[:, 0:H])
         nc.vector.tensor_scalar(sums[:, H:V], acc[1][:], bias[:], 0.0, ADD, MAX)
         nc.scalar.activation(result[:, H:V], sums[:, H:V], SQUARE)
-        nc.scalar.dma_start(out=out[:, H:V], in_=result[:, H:V])
+        nc.sync.dma_start(out=out[:, H:V], in_=result[:, H:V])

@@ -60,7 +60,6 @@ def tile_picked_deform_lin_relu2_def_e_kernel(tc, xT, w, b, offs, out):
 
         x_rows = xT.rearrange("(p j) c -> p j c", j=PACK)
         x_raw = []
-        nc.sync.dma_start(offsets[:], offs)
         for i, (u, c0, width, share) in enumerate(CHUNKS):
             if i == len(CHUNKS) - 2:
                 raw = shared.tile([P, 2, width], F32, name=f"x_raw{i}", offset=X_RAW_AT, align_bytes=64)
@@ -68,6 +67,8 @@ def tile_picked_deform_lin_relu2_def_e_kernel(tc, xT, w, b, offs, out):
                 raw = keep.tile([P, 2, width], F32, name=f"x_raw{i}")
             nc.sync.dma_start(out=raw[:], in_=x_rows[:, 2 * u : 2 * u + 2, c0 : c0 + width])
             x_raw.append(raw)
+            if i == 0:
+                nc.sync.dma_start(offsets[:], offs)
         w_raw = []
         for d in range(D):
             raw = shared.tile([P, PACK, N], F32, name=f"w_raw{d}", offset=W_RAW_AT[d], align_bytes=64)

@@ -24,7 +24,7 @@ CHUNKS = [
     (1, 0, 512, 0),
     (1, 512, 512, 0),
     (1, 1024, 512, 0),
-    (1, 1536, 512, 320),
+    (1, 1536, 512, 352),
 ]
 EARLY = 128
 EARLY_WINDOW = 8 * EARLY
@@ -53,6 +53,7 @@ def tile_picked_deform_lin_relu2_def_e_kernel(tc, xT, w, b, offs, out):
         w_codes = keep.tile([P, D * N], U32, name="w_codes", align_bytes=64)
         w_scales = keep.tile([P, D * N], U8, name="w_scales", align_bytes=64)
         on_vector = keep.tile([P, 8 * H], U32, name="x_on_vector", align_bytes=64)
+        early = keep.tile([P, 2, H, 2], U32, name="early", align_bytes=64)
         bias = keep.tile([P, 1], F32, name="bias")
         sums = keep.tile([P, V], F32, name="sums")
         result = keep.tile([P, V], F32, name="result")
@@ -82,11 +83,6 @@ def tile_picked_deform_lin_relu2_def_e_kernel(tc, xT, w, b, offs, out):
                     out=picked[:, u, c0 : c0 + e1 - e0], in_=pairs[u][:, 0:window].indirect(offsets[:, e0 // 16 : e1 // 16])
                 )
 
-        def weave_on_vector(dst, src):
-            nc.vector.tensor_copy(
-                out=dst.bitcast(I32).rearrange("p (v u) -> p v u", u=2), in_=src.bitcast(I32).rearrange("p u v -> p v u")
-            )
-
         def quantize(first, count, grouped):
             cols = slice(first * H, (first + count) * H)
             nc.vector.quantize_mx(
@@ -106,17 +102,17 @@ def tile_picked_deform_lin_relu2_def_e_kernel(tc, xT, w, b, offs, out):
                     in_=raw[:, :, 0:a].rearrange("p j c -> p c j"),
                 )
             if c0 + width == EARLY_WINDOW:
-                gather(u, EARLY_SLICES, EARLY_WINDOW)
-                if u == 1:
-                    for g in range(2):
-                        weave_on_vector(on_vector[:, 2 * g * H : 2 * (g + 1) * H], picked[:, :, g * H : (g + 1) * H])
+                for g, (e0, e1, unused) in enumerate(EARLY_SLICES):
+                    nc.vector.tensor_copy(
+                        out=early[:, g, :, u], in_=pairs[u][:, 0:EARLY_WINDOW].indirect(offsets[:, e0 // 16 : e1 // 16])
+                    )
             if c0 + width == T:
                 if u == 1:
                     early_codes = shared.tile([P, 2 * H], U32, name="early_codes", offset=X_RAW_AT, align_bytes=64)
                     nc.vector.quantize_mx(
                         out=early_codes[:].bitcast(FP8X4),
                         scales=x_scales[:, 0 : 2 * H],
-                        in_=on_vector[:, 0 : 4 * H].bitcast(BF16),
+                        in_=early[:].rearrange("p g v u -> p (g v u)").bitcast(BF16),
                     )
                 gather(u, LATE_SLICES, T)
 

@@ -14,17 +14,18 @@ U8 = mybir.dt.uint8
 FP8X4 = mybir.dt.float8_e4m3fn_x4
 ADD = mybir.AluOpType.add
 MAX = mybir.AluOpType.max
+MULT = mybir.AluOpType.mult
 SQUARE = mybir.ActivationFunctionType.Square
 
 P = 128
 PACK = 4
 CHUNKS = [
-    (0, 0, 1024, 1024),
-    (0, 1024, 1024, 704),
+    (0, 0, 1024, 704),
+    (0, 1024, 1024, 640),
     (1, 0, 512, 0),
     (1, 512, 512, 0),
     (1, 1024, 512, 0),
-    (1, 1536, 512, 352),
+    (1, 1536, 512, 288),
 ]
 EARLY = 128
 EARLY_WINDOW = 8 * EARLY
@@ -171,5 +172,5 @@ def tile_picked_deform_lin_relu2_def_e_kernel(tc, xT, w, b, offs, out):
         nc.scalar.activation(result[:, 0:H], sums[:, 0:H], SQUARE)
         nc.sync.dma_start(out=out[:, 0:H], in_=result[:, 0:H])
         nc.vector.tensor_scalar(sums[:, H:V], acc[1][:], bias[:], 0.0, ADD, MAX)
-        nc.scalar.activation(result[:, H:V], sums[:, H:V], SQUARE)
+        nc.vector.tensor_tensor(result[:, H:V], sums[:, H:V], sums[:, H:V], MULT)
         nc.sync.dma_start(out=out[:, H:V], in_=result[:, H:V])

@@ -30,13 +30,13 @@ CHUNKS = [
 EARLY = 128
 EARLY_WINDOW = 8 * EARLY
 EARLY_SLICES = [(0, EARLY, 0), (2 * V, 2 * V + EARLY, EARLY)]
-LATE_SLICES = [(2 * V + EARLY, S, 2 * V + EARLY), (EARLY, 2 * V, 2 * EARLY)]
+LATE_SLICES = [(EARLY, 2 * V, 2 * EARLY), (2 * V + EARLY, S, 2 * V + EARLY)]
 H = V // 2
-W_RAW_AT = [0, 2048, 4096, 6144, 9216]
-X_RAW_AT = 12288
-WOVEN_AT = [6144, 8192, 10240]
+W_RAW_AT = [0, 4096, 6272, 10240, 14336]
+X_RAW_AT = 16384
+ON_VECTOR_AT = 4160
+WOVEN_AT = [2112, 9280, 14336]
 RELU = mybir.ActivationFunctionType.Relu
-W_PARTS = [(0, 2), (2, 4), (4, 5)]
 
 
 def tile_picked_deform_lin_relu2_def_e_kernel(tc, xT, w, b, offs, out):
@@ -53,7 +53,6 @@ def tile_picked_deform_lin_relu2_def_e_kernel(tc, xT, w, b, offs, out):
         x_scales = keep.tile([P, S], U8, name="x_scales", align_bytes=64)
         w_codes = keep.tile([P, D * N], U32, name="w_codes", align_bytes=64)
         w_scales = keep.tile([P, D * N], U8, name="w_scales", align_bytes=64)
-        on_vector = keep.tile([P, 8 * H], U32, name="x_on_vector", align_bytes=64)
         early = keep.tile([P, 2, H, 2], U32, name="early", align_bytes=64)
         bias = keep.tile([P, 1], F32, name="bias")
         sums = keep.tile([P, V], F32, name="sums")
@@ -117,44 +116,57 @@ def tile_picked_deform_lin_relu2_def_e_kernel(tc, xT, w, b, offs, out):
                     )
                 gather(u, LATE_SLICES, T)
 
-        w_grouped = []
-        for i, (d0, d1) in enumerate(W_PARTS):
-            grouped = keep.tile([P, d1 - d0, N, PACK], BF16, name=f"w_grouped{i}", align_bytes=64)
+        def round_w(d0, d1):
+            grouped = keep.tile([P, d1 - d0, N, PACK], BF16, name=f"w_grouped{d0}", align_bytes=64)
             for d in range(d0, d1):
                 nc.scalar.copy(
                     out=grouped[:, d - d0].rearrange("p (c i) j -> p c j i", i=4),
                     in_=w_raw[d][:].rearrange("p j (c i) -> p c j i", i=4),
                 )
-            w_grouped.append(grouped)
-        for i, (d0, d1) in enumerate(W_PARTS):
             m_cols = slice(d0 * N, d1 * N)
             nc.vector.quantize_mx(
                 out=w_codes[:, m_cols].bitcast(FP8X4),
                 scales=w_scales[:, m_cols],
-                in_=w_grouped[i][:].rearrange("p d m j -> p (d m j)"),
+                in_=grouped[:].rearrange("p d m j -> p (d m j)"),
             )
 
+        def weave_on_scalar(i, src):
+            grouped = shared.tile([P, 4 * H], U32, name=f"x_on_scalar{i}", offset=WOVEN_AT[i], align_bytes=64)
+            nc.scalar.copy(out=grouped[:].rearrange("p (g v u) -> p g v u", g=2, u=2), in_=src)
+            return grouped
+
         blocks = picked[:].rearrange("p u (g v) -> p g v u", v=H)
+        round_w(0, 2)
+        on_vector = shared.tile([P, 4 * H], U32, name="x_on_vector", offset=ON_VECTOR_AT, align_bytes=64)
         nc.vector.tensor_copy(
-            out=on_vector[:, 4 * H : 8 * H].bitcast(I32).rearrange("p (g v u) -> p g v u", g=2, u=2),
-            in_=picked[:].bitcast(I32).rearrange("p u (g v) -> p g v u", v=H)[:, 6:9:2],
+            out=on_vector[:].bitcast(I32).rearrange("p (g v u) -> p g v u", g=2, u=2),
+            in_=picked[:].bitcast(I32).rearrange("p u (g v) -> p g v u", v=H)[:, 4:6],
         )
-        first_codes = shared.tile([P, 4 * H], U32, name="first_codes", offset=W_RAW_AT[2], align_bytes=64)
+        quantize(4, 2, weave_on_scalar(0, blocks[:, 2:4])[:])
+        w2 = keep.tile([P, 2, N, PACK], BF16, name="w_grouped2", align_bytes=64)
+        for d in (2, 3):
+            nc.scalar.copy(
+                out=w2[:, d - 2].rearrange("p (c i) j -> p c j i", i=4),
+                in_=w_raw[d][:].rearrange("p j (c i) -> p c j i", i=4),
+            )
+        first_codes = shared.tile([P, 4 * H], U32, name="first_codes", offset=W_RAW_AT[3] + 1088, align_bytes=64)
+        nc.vector.quantize_mx(
+            out=w_codes[:, 2 * N : 4 * N].bitcast(FP8X4),
+            scales=w_scales[:, 2 * N : 4 * N],
+            in_=w2[:].rearrange("p d m j -> p (d m j)"),
+        )
         nc.vector.quantize_mx(
             out=first_codes[:, 2 * H : 4 * H].bitcast(FP8X4),
             scales=x_scales[:, 2 * H : 4 * H],
-            in_=on_vector[:, 4 * H : 8 * H].bitcast(BF16),
+            in_=on_vector[:].bitcast(BF16),
         )
-        for i, src in enumerate([blocks[:, 7:10:2], blocks[:, 2:4], blocks[:, 4:6]]):
-            grouped = shared.tile([P, 4 * H], U32, name=f"x_on_scalar{i}", offset=WOVEN_AT[i], align_bytes=64)
-            nc.scalar.copy(out=grouped[:].rearrange("p (g v u) -> p g v u", g=2, u=2), in_=src)
-            if i < 2:
-                quantize(4 + 2 * i, 2, grouped[:])
-            else:
-                quantize(8, 1, grouped[:, 0 : 2 * H])
-                quantize(9, 1, grouped[:, 2 * H : 4 * H])
+        quantize(6, 2, weave_on_scalar(1, blocks[:, 6:9:2])[:])
+        round_w(4, 5)
+        last = weave_on_scalar(2, blocks[:, 7:10:2])
+        quantize(8, 1, last[:, 0 : 2 * H])
+        quantize(9, 1, last[:, 2 * H : 4 * H])
 
-        for h, taps in enumerate([[(0, 0), (2, 1), (3, 2), (4, 3), (1, 7)], [(3, 4), (4, 5), (0, 6), (1, 8), (2, 9)]]):
+        for h, taps in enumerate([[(0, 0), (1, 5), (2, 1), (3, 6), (4, 7)], [(0, 4), (1, 2), (2, 3), (3, 8), (4, 9)]]):
             for i, (d, block) in enumerate(taps):
                 m_cols = slice(d * N, (d + 1) * N)
                 cols = slice(block * H, (block + 1) * H)

@@ -29,13 +29,15 @@ CHUNKS = [
 ]
 EARLY = 128
 EARLY_WINDOW = 8 * EARLY
-EARLY_SLICES = [(0, EARLY, 0), (2 * V, 2 * V + EARLY, EARLY)]
-LATE_SLICES = [(EARLY, 2 * V, 2 * EARLY), (2 * V + EARLY, S, 2 * V + EARLY)]
 H = V // 2
-W_RAW_AT = [0, 4096, 6272, 10240, 14336]
-X_RAW_AT = 16384
-ON_VECTOR_AT = 4160
-WOVEN_AT = [2112, 9280, 14336]
+EARLY_SLICES = [(0, EARLY), (2 * V, 2 * V + EARLY)]
+RUN_A = (H, 2 * V, 0)
+RUN_B = (2 * V + H, 4 * V, 3 * H)
+RUN_C = (4 * V, S, 6 * H)
+RUN_BC = (2 * V + H, S, 3 * H)
+LATE_RUNS = [[RUN_A, RUN_BC], [RUN_C, RUN_A, RUN_B]]
+W_RAW_AT = {1: 0, 3: 8192}
+X_RAW_AT = 4096
 RELU = mybir.ActivationFunctionType.Relu
 
 
@@ -48,8 +50,8 @@ def tile_picked_deform_lin_relu2_def_e_kernel(tc, xT, w, b, offs, out):
 
         offsets = keep.tile([P, S // 16], U16, name="offsets")
         pairs = [keep.tile([P, T], U32, name=f"pairs{u}", align_bytes=64) for u in range(2)]
-        picked = keep.tile([P, 2, S], U32, name="picked", align_bytes=64)
-        x_codes = keep.tile([P, S], U32, name="x_codes", align_bytes=64)
+        picked = keep.tile([P, 2, 8 * H], U32, name="picked", align_bytes=64)
+        x_codes = keep.tile([P, 8 * H], U32, name="x_codes", align_bytes=64)
         x_scales = keep.tile([P, S], U8, name="x_scales", align_bytes=64)
         w_codes = keep.tile([P, D * N], U32, name="w_codes", align_bytes=64)
         w_scales = keep.tile([P, D * N], U8, name="w_scales", align_bytes=64)
@@ -72,22 +74,13 @@ def tile_picked_deform_lin_relu2_def_e_kernel(tc, xT, w, b, offs, out):
                 nc.sync.dma_start(offsets[:], offs)
         w_raw = []
         for d in range(D):
-            raw = shared.tile([P, PACK, N], F32, name=f"w_raw{d}", offset=W_RAW_AT[d], align_bytes=64)
+            if d in W_RAW_AT:
+                raw = shared.tile([P, PACK, N], F32, name=f"w_raw{d}", offset=W_RAW_AT[d], align_bytes=64)
+            else:
+                raw = keep.tile([P, PACK, N], F32, name=f"w_raw{d}", align_bytes=64)
             nc.sync.dma_start(out=raw[:], in_=w[d].rearrange("(p j) m -> p j m", j=PACK))
             w_raw.append(raw)
         nc.sync.dma_start(out=bias[:], in_=b)
-
-        def gather(u, slices, window):
-            for e0, e1, c0 in slices:
-                nc.vector.tensor_copy(
-                    out=picked[:, u, c0 : c0 + e1 - e0], in_=pairs[u][:, 0:window].indirect(offsets[:, e0 // 16 : e1 // 16])
-                )
-
-        def quantize(first, count, grouped):
-            cols = slice(first * H, (first + count) * H)
-            nc.vector.quantize_mx(
-                out=x_codes[:, cols].bitcast(FP8X4), scales=x_scales[:, cols], in_=grouped.bitcast(BF16)
-            )
 
         for i, (u, c0, width, a) in enumerate(CHUNKS):
             raw = x_raw[i]
@@ -102,7 +95,7 @@ def tile_picked_deform_lin_relu2_def_e_kernel(tc, xT, w, b, offs, out):
                     in_=raw[:, :, 0:a].rearrange("p j c -> p c j"),
                 )
             if c0 + width == EARLY_WINDOW:
-                for g, (e0, e1, unused) in enumerate(EARLY_SLICES):
+                for g, (e0, e1) in enumerate(EARLY_SLICES):
                     nc.vector.tensor_copy(
                         out=early[:, g, :, u], in_=pairs[u][:, 0:EARLY_WINDOW].indirect(offsets[:, e0 // 16 : e1 // 16])
                     )
@@ -111,70 +104,77 @@ def tile_picked_deform_lin_relu2_def_e_kernel(tc, xT, w, b, offs, out):
                     early_codes = shared.tile([P, 2 * H], U32, name="early_codes", offset=X_RAW_AT, align_bytes=64)
                     nc.vector.quantize_mx(
                         out=early_codes[:].bitcast(FP8X4),
-                        scales=x_scales[:, 0 : 2 * H],
+                        scales=x_scales[:, 8 * H : 10 * H],
                         in_=early[:].rearrange("p g v u -> p (g v u)").bitcast(BF16),
                     )
-                gather(u, LATE_SLICES, T)
+                for e0, e1, at in LATE_RUNS[u]:
+                    nc.vector.tensor_copy(
+                        out=picked[:, u, at : at + e1 - e0], in_=pairs[u][:].indirect(offsets[:, e0 // 16 : e1 // 16])
+                    )
 
-        def round_w(d0, d1):
-            grouped = keep.tile([P, d1 - d0, N, PACK], BF16, name=f"w_grouped{d0}", align_bytes=64)
-            for d in range(d0, d1):
-                nc.scalar.copy(
-                    out=grouped[:, d - d0].rearrange("p (c i) j -> p c j i", i=4),
-                    in_=w_raw[d][:].rearrange("p j (c i) -> p c j i", i=4),
-                )
-            m_cols = slice(d0 * N, d1 * N)
+        w_grouped = [keep.tile([P, n, N, PACK], BF16, name=f"w_grouped{i}", align_bytes=64) for i, n in enumerate((2, 2, 1))]
+
+        def round_w_on_scalar(d):
+            nc.scalar.copy(
+                out=w_grouped[d // 2][:, d % 2].rearrange("p (c i) j -> p c j i", i=4),
+                in_=w_raw[d][:].rearrange("p j (c i) -> p c j i", i=4),
+            )
+
+        def round_w_on_gpsimd(d):
+            nc.gpsimd.tensor_scalar(
+                w_grouped[d // 2][:, d % 2], w_raw[d][:].rearrange("p j m -> p m j"), 1.0, 0.0, MULT, ADD
+            )
+
+        def quantize_w(i):
+            m_cols = slice(2 * i * N, min(2 * i + 2, D) * N)
             nc.vector.quantize_mx(
                 out=w_codes[:, m_cols].bitcast(FP8X4),
                 scales=w_scales[:, m_cols],
-                in_=grouped[:].rearrange("p d m j -> p (d m j)"),
+                in_=w_grouped[i][:].rearrange("p d m j -> p (d m j)"),
             )
 
-        def weave_on_scalar(i, src):
-            grouped = shared.tile([P, 4 * H], U32, name=f"x_on_scalar{i}", offset=WOVEN_AT[i], align_bytes=64)
-            nc.scalar.copy(out=grouped[:].rearrange("p (g v u) -> p g v u", g=2, u=2), in_=src)
-            return grouped
+        def quantize_x(first, count, grouped):
+            cols = slice(first * H, (first + count) * H)
+            nc.vector.quantize_mx(out=x_codes[:, cols].bitcast(FP8X4), scales=x_scales[:, cols], in_=grouped.bitcast(BF16))
+
+        def weave_on_scalar(dst, src):
+            nc.scalar.copy(out=dst.rearrange("p (g v u) -> p g v u", v=H, u=2), in_=src)
 
         blocks = picked[:].rearrange("p u (g v) -> p g v u", v=H)
-        round_w(0, 2)
-        on_vector = shared.tile([P, 4 * H], U32, name="x_on_vector", offset=ON_VECTOR_AT, align_bytes=64)
+        round_w_on_scalar(0)
+        round_w_on_gpsimd(1)
+        round_w_on_gpsimd(2)
+        woven_c = keep.tile([P, 4 * H], U32, name="woven_c", align_bytes=64)
+        weave_on_scalar(woven_c[:], blocks[:, 6:8])
+        quantize_x(4, 2, woven_c[:])
+        quantize_w(0)
+        woven_a = shared.tile([P, 8 * H], U32, name="woven_a", offset=W_RAW_AT[1], align_bytes=64)
+        weave_on_scalar(woven_a[:, 0 : 6 * H], blocks[:, 0:3])
         nc.vector.tensor_copy(
-            out=on_vector[:].bitcast(I32).rearrange("p (g v u) -> p g v u", g=2, u=2),
-            in_=picked[:].bitcast(I32).rearrange("p u (g v) -> p g v u", v=H)[:, 4:6],
+            out=woven_a[:, 6 * H : 8 * H].bitcast(I32).rearrange("p (v u) -> p v u", u=2),
+            in_=picked[:].bitcast(I32).rearrange("p u c -> p c u")[:, 4 * H : 5 * H],
         )
-        quantize(4, 2, weave_on_scalar(0, blocks[:, 2:4])[:])
-        w2 = keep.tile([P, 2, N, PACK], BF16, name="w_grouped2", align_bytes=64)
-        for d in (2, 3):
-            nc.scalar.copy(
-                out=w2[:, d - 2].rearrange("p (c i) j -> p c j i", i=4),
-                in_=w_raw[d][:].rearrange("p j (c i) -> p c j i", i=4),
-            )
-        first_codes = shared.tile([P, 4 * H], U32, name="first_codes", offset=W_RAW_AT[3] + 1088, align_bytes=64)
-        nc.vector.quantize_mx(
-            out=w_codes[:, 2 * N : 4 * N].bitcast(FP8X4),
-            scales=w_scales[:, 2 * N : 4 * N],
-            in_=w2[:].rearrange("p d m j -> p (d m j)"),
-        )
-        nc.vector.quantize_mx(
-            out=first_codes[:, 2 * H : 4 * H].bitcast(FP8X4),
-            scales=x_scales[:, 2 * H : 4 * H],
-            in_=on_vector[:].bitcast(BF16),
-        )
-        quantize(6, 2, weave_on_scalar(1, blocks[:, 6:9:2])[:])
-        round_w(4, 5)
-        last = weave_on_scalar(2, blocks[:, 7:10:2])
-        quantize(8, 1, last[:, 0 : 2 * H])
-        quantize(9, 1, last[:, 2 * H : 4 * H])
+        quantize_x(0, 2, woven_a[:, 0 : 4 * H])
+        quantize_x(2, 2, woven_a[:, 4 * H : 8 * H])
+        round_w_on_scalar(3)
+        quantize_w(1)
+        round_w_on_scalar(4)
+        quantize_w(2)
+        woven_b = shared.tile([P, 4 * H], U32, name="woven_b", offset=W_RAW_AT[3], align_bytes=64)
+        weave_on_scalar(woven_b[:], blocks[:, 3:6:2])
+        quantize_x(6, 1, woven_b[:, 0 : 2 * H])
+        quantize_x(7, 1, woven_b[:, 2 * H : 4 * H])
 
-        for h, taps in enumerate([[(0, 0), (1, 5), (2, 1), (3, 6), (4, 7)], [(0, 4), (1, 2), (2, 3), (3, 8), (4, 9)]]):
+        for h, taps in enumerate([[(0, 8), (1, 1), (2, 9), (3, 3), (4, 4)], [(0, 0), (1, 2), (4, 5), (2, 6), (3, 7)]]):
             for i, (d, block) in enumerate(taps):
                 m_cols = slice(d * N, (d + 1) * N)
                 cols = slice(block * H, (block + 1) * H)
+                codes = x_codes[:, cols] if block < 8 else early_codes[:, (block - 8) * H : (block - 7) * H]
                 nc.tensor.matmul_mx(
                     out=acc[h][:],
                     lhsT=w_codes[:, m_cols].bitcast(FP8X4),
                     lhsT_scale=w_scales[:, m_cols],
-                    rhs=(early_codes if block < 2 else first_codes if block < 4 else x_codes)[:, cols].bitcast(FP8X4),
+                    rhs=codes.bitcast(FP8X4),
                     rhs_scale=x_scales[:, cols],
                     start=(i == 0),
                     stop=(i == D - 1),

@@ -19,6 +19,7 @@ SQUARE = mybir.ActivationFunctionType.Square
 
 P = 128
 PACK = 4
+H = V // 2
 CHUNKS = [
     (0, 0, 1024, 704),
     (0, 1024, 1024, 640),
@@ -27,17 +28,12 @@ CHUNKS = [
     (1, 1024, 512, 0),
     (1, 1536, 512, 288),
 ]
-EARLY = 128
-EARLY_WINDOW = 8 * EARLY
-H = V // 2
-EARLY_SLICES = [(0, EARLY), (2 * V, 2 * V + EARLY)]
-RUN_A = (H, 2 * V, 0)
-RUN_B = (2 * V + H, 4 * V, 3 * H)
-RUN_C = (4 * V, S, 6 * H)
-RUN_BC = (2 * V + H, S, 3 * H)
-LATE_RUNS = [[RUN_A, RUN_BC], [RUN_C, RUN_A, RUN_B]]
-W_RAW_AT = {1: 0, 3: 8192}
-X_RAW_AT = 4096
+EARLY_WINDOW = 8 * H
+EARLY_RUNS = [(0, H), (2 * V, 2 * V + H)]
+LATE_RUNS = [
+    [(H, 2 * V, 0), (2 * V + H, S, 3 * H)],
+    [(H, 2 * V, 0), (2 * V + H, 4 * V, 3 * H), (4 * V, S, 6 * H)],
+]
 RELU = mybir.ActivationFunctionType.Relu
 
 
@@ -50,22 +46,28 @@ def tile_picked_deform_lin_relu2_def_e_kernel(tc, xT, w, b, offs, out):
 
         offsets = keep.tile([P, S // 16], U16, name="offsets")
         pairs = [keep.tile([P, T], U32, name=f"pairs{u}", align_bytes=64) for u in range(2)]
+        early = keep.tile([P, 2, H, 2], U32, name="early", align_bytes=64)
         picked = keep.tile([P, 2, 8 * H], U32, name="picked", align_bytes=64)
+        woven = keep.tile([P, 4 * V], U32, name="woven", align_bytes=64)
         x_codes = keep.tile([P, 8 * H], U32, name="x_codes", align_bytes=64)
         x_scales = keep.tile([P, S], U8, name="x_scales", align_bytes=64)
+        w_grouped = keep.tile([P, D * N * PACK], BF16, name="w_grouped", align_bytes=64)
         w_codes = keep.tile([P, D * N], U32, name="w_codes", align_bytes=64)
         w_scales = keep.tile([P, D * N], U8, name="w_scales", align_bytes=64)
-        early = keep.tile([P, 2, H, 2], U32, name="early", align_bytes=64)
         bias = keep.tile([P, 1], F32, name="bias")
         sums = keep.tile([P, V], F32, name="sums")
         result = keep.tile([P, V], F32, name="result")
         acc = [psum.tile([P, H], F32, name=f"acc{h}") for h in range(2)]
 
+        one = keep.tile([P, 1], F32, name="one")
+        zero = keep.tile([P, 1], F32, name="zero")
+        nc.gpsimd.memset(one[:], 1.0)
+        nc.gpsimd.tensor_scalar(zero[:], one[:], 0.0, 0.0, MULT, ADD)
         x_rows = xT.rearrange("(p j) c -> p j c", j=PACK)
         x_raw = []
         for i, (u, c0, width, share) in enumerate(CHUNKS):
             if i == len(CHUNKS) - 2:
-                raw = shared.tile([P, 2, width], F32, name=f"x_raw{i}", offset=X_RAW_AT, align_bytes=64)
+                raw = shared.tile([P, 2, width], F32, name=f"x_raw{i}", offset=0, align_bytes=64)
             else:
                 raw = keep.tile([P, 2, width], F32, name=f"x_raw{i}")
             nc.sync.dma_start(out=raw[:], in_=x_rows[:, 2 * u : 2 * u + 2, c0 : c0 + width])
@@ -74,34 +76,29 @@ def tile_picked_deform_lin_relu2_def_e_kernel(tc, xT, w, b, offs, out):
                 nc.sync.dma_start(offsets[:], offs)
         w_raw = []
         for d in range(D):
-            if d in W_RAW_AT:
-                raw = shared.tile([P, PACK, N], F32, name=f"w_raw{d}", offset=W_RAW_AT[d], align_bytes=64)
-            else:
-                raw = keep.tile([P, PACK, N], F32, name=f"w_raw{d}", align_bytes=64)
-            nc.sync.dma_start(out=raw[:], in_=w[d].rearrange("(p j) m -> p j m", j=PACK))
+            raw = keep.tile([P, PACK * N], F32, name=f"w_raw{d}", align_bytes=64)
+            nc.sync.dma_start(out=raw[:], in_=w[d].rearrange("(p j) m -> p (j m)", j=PACK))
             w_raw.append(raw)
         nc.sync.dma_start(out=bias[:], in_=b)
 
         for i, (u, c0, width, a) in enumerate(CHUNKS):
-            raw = x_raw[i]
-            if a < width:
-                nc.scalar.copy(
-                    out=pairs[u][:, c0 + a : c0 + width].bitcast(BF16).rearrange("p (c j) -> p c j", j=2),
-                    in_=raw[:, :, a:width].rearrange("p j c -> p c j"),
-                )
+            nc.scalar.copy(
+                out=pairs[u][:, c0 + a : c0 + width].bitcast(BF16).rearrange("p (c j) -> p c j", j=2),
+                in_=x_raw[i][:, :, a:width].rearrange("p j c -> p c j"),
+            )
             if a > 0:
                 nc.vector.tensor_copy(
                     out=pairs[u][:, c0 : c0 + a].bitcast(BF16).rearrange("p (c j) -> p c j", j=2),
-                    in_=raw[:, :, 0:a].rearrange("p j c -> p c j"),
+                    in_=x_raw[i][:, :, 0:a].rearrange("p j c -> p c j"),
                 )
             if c0 + width == EARLY_WINDOW:
-                for g, (e0, e1) in enumerate(EARLY_SLICES):
+                for g, (e0, e1) in enumerate(EARLY_RUNS):
                     nc.vector.tensor_copy(
                         out=early[:, g, :, u], in_=pairs[u][:, 0:EARLY_WINDOW].indirect(offsets[:, e0 // 16 : e1 // 16])
                     )
             if c0 + width == T:
                 if u == 1:
-                    early_codes = shared.tile([P, 2 * H], U32, name="early_codes", offset=X_RAW_AT, align_bytes=64)
+                    early_codes = shared.tile([P, 2 * H], U32, name="early_codes", offset=0, align_bytes=64)
                     nc.vector.quantize_mx(
                         out=early_codes[:].bitcast(FP8X4),
                         scales=x_scales[:, 8 * H : 10 * H],
@@ -112,61 +109,52 @@ def tile_picked_deform_lin_relu2_def_e_kernel(tc, xT, w, b, offs, out):
                         out=picked[:, u, at : at + e1 - e0], in_=pairs[u][:].indirect(offsets[:, e0 // 16 : e1 // 16])
                     )
 
-        w_grouped = [keep.tile([P, n, N, PACK], BF16, name=f"w_grouped{i}", align_bytes=64) for i, n in enumerate((2, 2, 1))]
-
-        def round_w_on_scalar(d):
+        def round_w(d):
+            grouped = w_grouped[:, d * N * PACK : (d + 1) * N * PACK]
             nc.scalar.copy(
-                out=w_grouped[d // 2][:, d % 2].rearrange("p (c i) j -> p c j i", i=4),
-                in_=w_raw[d][:].rearrange("p j (c i) -> p c j i", i=4),
+                out=grouped.rearrange("p (c i j) -> p c j i", i=4, j=PACK),
+                in_=w_raw[d][:].rearrange("p (j c i) -> p c j i", i=4, j=PACK),
             )
 
-        def round_w_on_gpsimd(d):
-            nc.gpsimd.tensor_scalar(
-                w_grouped[d // 2][:, d % 2], w_raw[d][:].rearrange("p j m -> p m j"), 1.0, 0.0, MULT, ADD
-            )
-
-        def quantize_w(i):
-            m_cols = slice(2 * i * N, min(2 * i + 2, D) * N)
+        def quantize_w(d0, d1):
+            m_cols = slice(d0 * N, d1 * N)
             nc.vector.quantize_mx(
                 out=w_codes[:, m_cols].bitcast(FP8X4),
                 scales=w_scales[:, m_cols],
-                in_=w_grouped[i][:].rearrange("p d m j -> p (d m j)"),
+                in_=w_grouped[:, d0 * N * PACK : d1 * N * PACK],
             )
 
-        def quantize_x(first, count, grouped):
+        def weave(copy, dst, first, count):
+            copy(
+                out=dst.rearrange("p (v u) -> p v u", u=2),
+                in_=picked[:].rearrange("p u c -> p c u")[:, first * H : (first + count) * H],
+            )
+
+        def quantize_x(first, count, src):
             cols = slice(first * H, (first + count) * H)
-            nc.vector.quantize_mx(out=x_codes[:, cols].bitcast(FP8X4), scales=x_scales[:, cols], in_=grouped.bitcast(BF16))
+            nc.vector.quantize_mx(out=x_codes[:, cols].bitcast(FP8X4), scales=x_scales[:, cols], in_=src.bitcast(BF16))
 
-        def weave_on_scalar(dst, src):
-            nc.scalar.copy(out=dst.rearrange("p (g v u) -> p g v u", v=H, u=2), in_=src)
+        weave(nc.gpsimd.tensor_copy, woven[:, 0 : 3 * V], 0, 3)
+        weave(nc.gpsimd.tensor_copy, woven[:, 3 * V : 4 * V], 3, 1)
+        for d in range(3):
+            round_w(d)
+        weave(nc.scalar.copy, w_raw[2][:].bitcast(U32), 4, 2)
+        quantize_w(0, 2)
+        quantize_x(0, 2, woven[:, 0 : 2 * V])
+        quantize_x(2, 2, woven[:, 2 * V : 4 * V])
+        round_w(3)
+        quantize_w(2, 4)
+        quantize_x(4, 2, w_raw[2][:])
+        round_w(4)
+        quantize_w(4, 5)
+        for h in range(2):
+            last = w_raw[3][:, h * V : (h + 1) * V]
+            weave(nc.scalar.copy, last.bitcast(U32), 6 + h, 1)
+            quantize_x(6 + h, 1, last)
 
-        blocks = picked[:].rearrange("p u (g v) -> p g v u", v=H)
-        round_w_on_scalar(0)
-        round_w_on_gpsimd(1)
-        round_w_on_gpsimd(2)
-        woven_c = keep.tile([P, 4 * H], U32, name="woven_c", align_bytes=64)
-        weave_on_scalar(woven_c[:], blocks[:, 6:8])
-        quantize_x(4, 2, woven_c[:])
-        quantize_w(0)
-        woven_a = shared.tile([P, 8 * H], U32, name="woven_a", offset=W_RAW_AT[1], align_bytes=64)
-        weave_on_scalar(woven_a[:, 0 : 6 * H], blocks[:, 0:3])
-        nc.vector.tensor_copy(
-            out=woven_a[:, 6 * H : 8 * H].bitcast(I32).rearrange("p (v u) -> p v u", u=2),
-            in_=picked[:].bitcast(I32).rearrange("p u c -> p c u")[:, 4 * H : 5 * H],
-        )
-        quantize_x(0, 2, woven_a[:, 0 : 4 * H])
-        quantize_x(2, 2, woven_a[:, 4 * H : 8 * H])
-        round_w_on_scalar(3)
-        quantize_w(1)
-        round_w_on_scalar(4)
-        quantize_w(2)
-        woven_b = shared.tile([P, 4 * H], U32, name="woven_b", offset=W_RAW_AT[3], align_bytes=64)
-        weave_on_scalar(woven_b[:], blocks[:, 3:6:2])
-        quantize_x(6, 1, woven_b[:, 0 : 2 * H])
-        quantize_x(7, 1, woven_b[:, 2 * H : 4 * H])
-
-        for h, taps in enumerate([[(0, 8), (1, 1), (2, 9), (3, 3), (4, 4)], [(0, 0), (1, 2), (4, 5), (2, 6), (3, 7)]]):
-            for i, (d, block) in enumerate(taps):
+        for d in range(D):
+            for h in range(2):
+                block = [[8, 1, 9, 4, 6], [0, 2, 3, 5, 7]][h][d]
                 m_cols = slice(d * N, (d + 1) * N)
                 cols = slice(block * H, (block + 1) * H)
                 codes = x_codes[:, cols] if block < 8 else early_codes[:, (block - 8) * H : (block - 7) * H]
@@ -176,13 +164,13 @@ def tile_picked_deform_lin_relu2_def_e_kernel(tc, xT, w, b, offs, out):
                     lhsT_scale=w_scales[:, m_cols],
                     rhs=codes.bitcast(FP8X4),
                     rhs_scale=x_scales[:, cols],
-                    start=(i == 0),
-                    stop=(i == D - 1),
+                    start=(d == 0),
+                    stop=(d == D - 1),
                 )
 
         nc.scalar.activation(sums[:, 0:H], acc[0][:], RELU, bias=bias[:])
         nc.scalar.activation(result[:, 0:H], sums[:, 0:H], SQUARE)
         nc.sync.dma_start(out=out[:, 0:H], in_=result[:, 0:H])
-        nc.vector.tensor_scalar(sums[:, H:V], acc[1][:], bias[:], 0.0, ADD, MAX)
+        nc.vector.tensor_scalar(sums[:, H:V], acc[1][:], bias[:], zero[:], ADD, MAX)
         nc.vector.tensor_tensor(result[:, H:V], sums[:, H:V], sums[:, H:V], MULT)
         nc.sync.dma_start(out=out[:, H:V], in_=result[:, H:V])

@@ -48,7 +48,8 @@ def tile_picked_deform_lin_relu2_def_e_kernel(tc, xT, w, b, offs, out):
         pairs = [keep.tile([P, T], U32, name=f"pairs{u}", align_bytes=64) for u in range(2)]
         early = keep.tile([P, 2, H, 2], U32, name="early", align_bytes=64)
         picked = keep.tile([P, 2, 8 * H], U32, name="picked", align_bytes=64)
-        woven = keep.tile([P, 4 * V], U32, name="woven", align_bytes=64)
+        woven = keep.tile([P, 3 * V], U32, name="woven", align_bytes=64)
+        behind_tap2 = keep.tile([P, 3 * V], F32, name="behind_tap2", align_bytes=64)
         x_codes = keep.tile([P, 8 * H], U32, name="x_codes", align_bytes=64)
         x_scales = keep.tile([P, S], U8, name="x_scales", align_bytes=64)
         w_grouped = keep.tile([P, D * N * PACK], BF16, name="w_grouped", align_bytes=64)
@@ -76,8 +77,11 @@ def tile_picked_deform_lin_relu2_def_e_kernel(tc, xT, w, b, offs, out):
                 nc.sync.dma_start(offsets[:], offs)
         w_raw = []
         for d in range(D):
-            raw = keep.tile([P, PACK * N], F32, name=f"w_raw{d}", align_bytes=64)
-            nc.sync.dma_start(out=raw[:], in_=w[d].rearrange("(p j) m -> p (j m)", j=PACK))
+            if d == 2:
+                raw = behind_tap2[:, 0 : PACK * N]
+            else:
+                raw = keep.tile([P, PACK * N], F32, name=f"w_raw{d}", align_bytes=64)[:]
+            nc.sync.dma_start(out=raw, in_=w[d].rearrange("(p j) m -> p (j m)", j=PACK))
             w_raw.append(raw)
         nc.sync.dma_start(out=bias[:], in_=b)
 
@@ -113,7 +117,7 @@ def tile_picked_deform_lin_relu2_def_e_kernel(tc, xT, w, b, offs, out):
             grouped = w_grouped[:, d * N * PACK : (d + 1) * N * PACK]
             nc.scalar.copy(
                 out=grouped.rearrange("p (c i j) -> p c j i", i=4, j=PACK),
-                in_=w_raw[d][:].rearrange("p (j c i) -> p c j i", i=4, j=PACK),
+                in_=w_raw[d].rearrange("p (j c i) -> p c j i", i=4, j=PACK),
             )
 
         def quantize_w(d0, d1):
@@ -135,16 +139,16 @@ def tile_picked_deform_lin_relu2_def_e_kernel(tc, xT, w, b, offs, out):
             nc.vector.quantize_mx(out=x_codes[:, cols].bitcast(FP8X4), scales=x_scales[:, cols], in_=src.bitcast(BF16))
 
         weave(nc.gpsimd.tensor_copy, woven[:, 0 : 3 * V], 0, 3)
-        weave(nc.gpsimd.tensor_copy, woven[:, 3 * V : 4 * V], 3, 1)
         for d in range(3):
             round_w(d)
-        weave(nc.scalar.copy, w_raw[2][:].bitcast(U32), 4, 2)
+        weave(nc.scalar.copy, behind_tap2[:, 0 : 3 * V].bitcast(U32), 3, 3)
         quantize_w(0, 2)
         quantize_x(0, 2, woven[:, 0 : 2 * V])
-        quantize_x(2, 2, woven[:, 2 * V : 4 * V])
+        quantize_x(2, 1, woven[:, 2 * V : 3 * V])
         round_w(3)
+        quantize_x(3, 2, behind_tap2[:, 0 : 2 * V])
         quantize_w(2, 4)
-        quantize_x(4, 2, w_raw[2][:])
+        quantize_x(5, 1, behind_tap2[:, 2 * V : 3 * V])
         round_w(4)
         quantize_w(4, 5)
         for h in range(2):

@@ -57,13 +57,9 @@ def tile_picked_deform_lin_relu2_def_e_kernel(tc, xT, w, b, offs, out):
         w_scales = keep.tile([P, D * N], U8, name="w_scales", align_bytes=64)
         bias = keep.tile([P, 1], F32, name="bias")
         sums = keep.tile([P, V], F32, name="sums")
-        result = keep.tile([P, V], F32, name="result")
+        result = keep.tile([P, V + 16], F32, name="result")
         acc = [psum.tile([P, H], F32, name=f"acc{h}") for h in range(2)]
 
-        one = keep.tile([P, 1], F32, name="one")
-        zero = keep.tile([P, 1], F32, name="zero")
-        nc.gpsimd.memset(one[:], 1.0)
-        nc.gpsimd.tensor_scalar(zero[:], one[:], 0.0, 0.0, MULT, ADD)
         x_rows = xT.rearrange("(p j) c -> p j c", j=PACK)
         x_raw = []
         for i, (u, c0, width, share) in enumerate(CHUNKS):
@@ -175,6 +171,6 @@ def tile_picked_deform_lin_relu2_def_e_kernel(tc, xT, w, b, offs, out):
         nc.scalar.activation(sums[:, 0:H], acc[0][:], RELU, bias=bias[:])
         nc.scalar.activation(result[:, 0:H], sums[:, 0:H], SQUARE)
         nc.sync.dma_start(out=out[:, 0:H], in_=result[:, 0:H])
-        nc.vector.tensor_scalar(sums[:, H:V], acc[1][:], bias[:], zero[:], ADD, MAX)
+        nc.vector.tensor_scalar(sums[:, H:V], acc[1][:], bias[:], 0.0, ADD, MAX)
         nc.vector.tensor_tensor(result[:, H:V], sums[:, H:V], sums[:, H:V], MULT)
         nc.sync.dma_start(out=out[:, H:V], in_=result[:, H:V])

@@ -23,8 +23,7 @@ H = V // 2
 CHUNKS = [
     (0, 0, 1024, 704),
     (0, 1024, 1024, 640),
-    (1, 0, 512, 0),
-    (1, 512, 512, 0),
+    (1, 0, 1024, 512),
     (1, 1024, 512, 0),
     (1, 1536, 512, 288),
 ]
@@ -87,7 +86,7 @@ def tile_picked_deform_lin_relu2_def_e_kernel(tc, xT, w, b, offs, out):
                 in_=x_raw[i][:, :, a:width].rearrange("p j c -> p c j"),
             )
             if a > 0:
-                nc.vector.tensor_copy(
+                (nc.gpsimd if i == 2 else nc.vector).tensor_copy(
                     out=pairs[u][:, c0 : c0 + a].bitcast(BF16).rearrange("p (c j) -> p c j", j=2),
                     in_=x_raw[i][:, :, 0:a].rearrange("p j c -> p c j"),
                 )

from contextlib import ExitStack

import concourse.mybir as mybir

K, T, D, S, V, N = 512, 2048, 5, 1280, 256, 128
FLOPS = 2 * N * V * D * K

F32 = mybir.dt.float32
BF16 = mybir.dt.bfloat16
U32 = mybir.dt.uint32
I32 = mybir.dt.int32
U16 = mybir.dt.uint16
U8 = mybir.dt.uint8
FP8X4 = mybir.dt.float8_e4m3fn_x4
ADD = mybir.AluOpType.add
MAX = mybir.AluOpType.max
MULT = mybir.AluOpType.mult
SQUARE = mybir.ActivationFunctionType.Square

P = 128
PACK = 4
H = V // 2
CHUNKS = [
    (0, 0, 1024, 704),
    (0, 1024, 1024, 640),
    (1, 0, 1024, 512),
    (1, 1024, 512, 0),
    (1, 1536, 512, 288),
]
EARLY_WINDOW = 8 * H
EARLY_RUNS = [(0, H), (2 * V, 2 * V + H)]
LATE_RUNS = [
    [(H, 2 * V, 0), (2 * V + H, S, 3 * H)],
    [(H, 2 * V, 0), (2 * V + H, 4 * V, 3 * H), (4 * V, S, 6 * H)],
]
RELU = mybir.ActivationFunctionType.Relu


def tile_picked_deform_lin_relu2_def_e_kernel(tc, xT, w, b, offs, out):
    nc = tc.nc
    with ExitStack() as ctx:
        keep = ctx.enter_context(tc.tile_pool(name="keep", bufs=1))
        shared = ctx.enter_context(tc.tile_pool(name="shared", bufs=1))
        psum = ctx.enter_context(tc.psum_pool(name="psum", bufs=1))

        offsets = keep.tile([P, S // 16], U16, name="offsets")
        pairs = [keep.tile([P, T], U32, name=f"pairs{u}", align_bytes=64) for u in range(2)]
        early = keep.tile([P, 2, H, 2], U32, name="early", align_bytes=64)
        picked = keep.tile([P, 2, 8 * H], U32, name="picked", align_bytes=64)
        woven = keep.tile([P, 3 * V], U32, name="woven", align_bytes=64)
        behind_tap2 = keep.tile([P, 3 * V], F32, name="behind_tap2", align_bytes=64)
        x_codes = keep.tile([P, 8 * H], U32, name="x_codes", align_bytes=64)
        x_scales = keep.tile([P, S], U8, name="x_scales", align_bytes=64)
        w_grouped = keep.tile([P, D * N * PACK], BF16, name="w_grouped", align_bytes=64)
        w_codes = keep.tile([P, D * N], U32, name="w_codes", align_bytes=64)
        w_scales = keep.tile([P, D * N], U8, name="w_scales", align_bytes=64)
        bias = keep.tile([P, 1], F32, name="bias")
        sums = keep.tile([P, V], F32, name="sums")
        result = keep.tile([P, V + 16], F32, name="result")
        acc = [psum.tile([P, H], F32, name=f"acc{h}") for h in range(2)]

        x_rows = xT.rearrange("(p j) c -> p j c", j=PACK)
        x_raw = []
        for i, (u, c0, width, share) in enumerate(CHUNKS):
            if i == len(CHUNKS) - 2:
                raw = shared.tile([P, 2, width], F32, name=f"x_raw{i}", offset=0, align_bytes=64)
            else:
                raw = keep.tile([P, 2, width], F32, name=f"x_raw{i}")
            nc.sync.dma_start(out=raw[:], in_=x_rows[:, 2 * u : 2 * u + 2, c0 : c0 + width])
            x_raw.append(raw)
            if i == 0:
                nc.sync.dma_start(offsets[:], offs)
        w_raw = []
        for d in range(D):
            if d == 2:
                raw = behind_tap2[:, 0 : PACK * N]
            else:
                raw = keep.tile([P, PACK * N], F32, name=f"w_raw{d}", align_bytes=64)[:]
            nc.sync.dma_start(out=raw, in_=w[d].rearrange("(p j) m -> p (j m)", j=PACK))
            w_raw.append(raw)
        nc.sync.dma_start(out=bias[:], in_=b)

        for i, (u, c0, width, a) in enumerate(CHUNKS):
            nc.scalar.copy(
                out=pairs[u][:, c0 + a : c0 + width].bitcast(BF16).rearrange("p (c j) -> p c j", j=2),
                in_=x_raw[i][:, :, a:width].rearrange("p j c -> p c j"),
            )
            if a > 0:
                (nc.gpsimd if i == 2 else nc.vector).tensor_copy(
                    out=pairs[u][:, c0 : c0 + a].bitcast(BF16).rearrange("p (c j) -> p c j", j=2),
                    in_=x_raw[i][:, :, 0:a].rearrange("p j c -> p c j"),
                )
            if c0 + width == EARLY_WINDOW:
                for g, (e0, e1) in enumerate(EARLY_RUNS):
                    nc.vector.tensor_copy(
                        out=early[:, g, :, u], in_=pairs[u][:, 0:EARLY_WINDOW].indirect(offsets[:, e0 // 16 : e1 // 16])
                    )
            if c0 + width == T:
                if u == 1:
                    early_codes = shared.tile([P, 2 * H], U32, name="early_codes", offset=0, align_bytes=64)
                    nc.vector.quantize_mx(
                        out=early_codes[:].bitcast(FP8X4),
                        scales=x_scales[:, 8 * H : 10 * H],
                        in_=early[:].rearrange("p g v u -> p (g v u)").bitcast(BF16),
                    )
                for e0, e1, at in LATE_RUNS[u]:
                    nc.vector.tensor_copy(
                        out=picked[:, u, at : at + e1 - e0], in_=pairs[u][:].indirect(offsets[:, e0 // 16 : e1 // 16])
                    )

        def round_w(d):
            grouped = w_grouped[:, d * N * PACK : (d + 1) * N * PACK]
            nc.scalar.copy(
                out=grouped.rearrange("p (c i j) -> p c j i", i=4, j=PACK),
                in_=w_raw[d].rearrange("p (j c i) -> p c j i", i=4, j=PACK),
            )

        def quantize_w(d0, d1):
            m_cols = slice(d0 * N, d1 * N)
            nc.vector.quantize_mx(
                out=w_codes[:, m_cols].bitcast(FP8X4),
                scales=w_scales[:, m_cols],
                in_=w_grouped[:, d0 * N * PACK : d1 * N * PACK],
            )

        def weave(copy, dst, first, count):
            copy(
                out=dst.rearrange("p (v u) -> p v u", u=2),
                in_=picked[:].rearrange("p u c -> p c u")[:, first * H : (first + count) * H],
            )

        def quantize_x(first, count, src):
            cols = slice(first * H, (first + count) * H)
            nc.vector.quantize_mx(out=x_codes[:, cols].bitcast(FP8X4), scales=x_scales[:, cols], in_=src.bitcast(BF16))

        weave(nc.gpsimd.tensor_copy, woven[:, 0 : 3 * V], 0, 3)
        for d in range(3):
            round_w(d)
        weave(nc.scalar.copy, behind_tap2[:, 0 : 3 * V].bitcast(U32), 3, 3)
        quantize_w(0, 2)
        quantize_x(0, 2, woven[:, 0 : 2 * V])
        quantize_x(2, 1, woven[:, 2 * V : 3 * V])
        round_w(3)
        quantize_x(3, 2, behind_tap2[:, 0 : 2 * V])
        quantize_w(2, 4)
        quantize_x(5, 1, behind_tap2[:, 2 * V : 3 * V])
        round_w(4)
        quantize_w(4, 5)
        for h in range(2):
            last = w_raw[3][:, h * V : (h + 1) * V]
            weave(nc.scalar.copy, last.bitcast(U32), 6 + h, 1)
            quantize_x(6 + h, 1, last)

        for d in range(D):
            for h in range(2):
                block = [[8, 1, 9, 4, 6], [0, 2, 3, 5, 7]][h][d]
                m_cols = slice(d * N, (d + 1) * N)
                cols = slice(block * H, (block + 1) * H)
                codes = x_codes[:, cols] if block < 8 else early_codes[:, (block - 8) * H : (block - 7) * H]
                nc.tensor.matmul_mx(
                    out=acc[h][:],
                    lhsT=w_codes[:, m_cols].bitcast(FP8X4),
                    lhsT_scale=w_scales[:, m_cols],
                    rhs=codes.bitcast(FP8X4),
                    rhs_scale=x_scales[:, cols],
                    start=(d == 0),
                    stop=(d == D - 1),
                )

        nc.scalar.activation(sums[:, 0:H], acc[0][:], RELU, bias=bias[:])
        nc.scalar.activation(result[:, 0:H], sums[:, 0:H], SQUARE)
        nc.sync.dma_start(out=out[:, 0:H], in_=result[:, 0:H])
        nc.vector.tensor_scalar(sums[:, H:V], acc[1][:], bias[:], 0.0, ADD, MAX)
        nc.vector.tensor_tensor(result[:, H:V], sums[:, H:V], sums[:, H:V], MULT)
        nc.sync.dma_start(out=out[:, H:V], in_=result[:, H:V])
